import numpy as np
import ml_dtypes


def mxq(x, axis, fmt="e4m3"):
    dtype, down = {"e4m3": (ml_dtypes.float8_e4m3fn, 7), "e5m2": (ml_dtypes.float8_e5m2, 14)}[fmt]
    v = np.moveaxis(np.asarray(x, np.float32).astype(ml_dtypes.bfloat16).astype(np.float64), axis, -1)
    blocks = v.reshape(v.shape[:-1] + (-1, 32))
    amax = np.abs(blocks).max(-1, keepdims=True)
    byte = np.maximum(np.where(amax > 0, np.frexp(amax)[1] - 1 + 127, 0) - down, 1)
    scale = np.exp2(byte - 127.0)
    codes = (blocks / scale).astype(np.float32).astype(dtype).astype(np.float64)
    return np.moveaxis((codes * scale).reshape(v.shape), -1, axis)


WIDE = False


def mx_kscale(k):
    if not WIDE:
        return np.ones(k)
    levels = np.array([10, -10, 5, -5, 0])
    if k % 512:
        return np.exp2(np.random.permutation(np.resize(levels, k // 32))).repeat(32)
    a = np.empty((k // 512, 16))
    for p in range(k // 512):
        a[p, :8] = np.random.permutation(np.resize(levels, 8))
        for g in range(8):
            far = levels[np.abs(levels - a[p, g]) >= 10]
            a[p, g + 8] = far[np.random.randint(len(far))]
    return np.exp2(a.ravel()).repeat(32)


def f64(x):
    return np.asarray(x).astype(np.float64)


def striped(idx):
    return np.tile(np.asarray(idx).reshape(-1, 16).T, (8, 1)).astype(np.uint16)


def unstriped(offs):
    return offs[:16].T.reshape(-1).astype(np.int64)


B, N, T, D, NQ = 1, 512, 2048, 512, 256
DV = 512


def setup_inputs():
    n = np.random.standard_normal
    pages = np.random.permutation(T // 16)[:B * N // 16]
    idx = (pages[:, None] * 16 + np.arange(16)[None, :]).reshape(-1)
    u = mx_kscale(N)
    ut = np.ones(T)
    ut[idx] = u
    return {
        "vT": (n((DV, T)) / ut).astype(np.float32),
        "wT": (np.random.dirichlet(np.ones(N), NQ).T[None] * u[:, None] * 16).astype(np.float32),
        "tg": (n((B, NQ, DV))).astype(np.float32),
        "offs": striped(idx),
    }


def reference(vT, wT, tg, offs):
    idx = unstriped(offs)
    pick = lambda x, which: x[:, which].reshape(x.shape[0], B, -1).transpose(1, 0, 2)
    wq = mxq(f64(wT), 1, "e4m3")
    o = wq.transpose(0, 2, 1) @ mxq(pick(f64(vT), idx).transpose(0, 2, 1), 1, "e4m3")
    r_ = np.square(o - f64(tg))
    return r_

@@ -1,0 +1,117 @@
+from contextlib import ExitStack
+
+import concourse.mybir as mybir
+from concourse.masks import make_identity
+
+SLOTS, TOKENS, QUERIES, FEATURES = 512, 2048, 256, 512
+FLOPS = 2 * QUERIES * SLOTS * FEATURES
+
+F32 = mybir.dt.float32
+BF16 = mybir.dt.bfloat16
+U32 = mybir.dt.uint32
+U16 = mybir.dt.uint16
+U8 = mybir.dt.uint8
+FP8X4 = mybir.dt.float8_e4m3fn_x4
+ACT = mybir.ActivationFunctionType
+ALU = mybir.AluOpType
+
+P = 128
+BLOCKS = FEATURES // P
+HALVES = QUERIES // P
+
+
+def tile_attend_wsum_dist_f_kernel(tc, vT, wT, tg, offs, out):
+    nc = tc.nc
+    with ExitStack() as ctx:
+        keep = ctx.enter_context(tc.tile_pool(name="keep", bufs=1))
+        ring = ctx.enter_context(tc.tile_pool(name="ring", bufs=2))
+        turn = ctx.enter_context(tc.psum_pool(name="turn", bufs=2))
+        sums = ctx.enter_context(tc.psum_pool(name="sums", bufs=1))
+
+        offsets = keep.tile([P, SLOTS // 16], U16, name="offsets")
+        pools = [keep.tile([P, TOKENS], F32, name="pool%d" % b) for b in range(BLOCKS)]
+        w_raw = keep.tile([P, 4, QUERIES], F32, name="w_raw")
+        tg_sb = [keep.tile([P, HALVES, 2 * P], F32, name="tg%d" % c) for c in range(2)]
+        tg_rows = tg[0].rearrange("(h p) e -> p h e", p=P)
+        out_rows = out[0].rearrange("(h p) e -> p h e", p=P)
+
+        nc.sync.dma_start(out=pools[0][:], in_=vT[0:P, :])
+        nc.sync.dma_start(offsets[:], offs)
+        nc.sync.dma_start(out=w_raw[:], in_=wT[0].rearrange("(p j) q -> p j q", j=4))
+        for b in range(1, BLOCKS):
+            nc.sync.dma_start(out=pools[b][:], in_=vT[b * P : (b + 1) * P, :])
+        for c in range(2):
+            nc.sync.dma_start(out=tg_sb[c][:], in_=tg_rows[:, :, c * 2 * P : (c + 1) * 2 * P])
+
+        ident = keep.tile([P, P], F32, name="ident")
+        make_identity(nc, ident[:])
+
+        w_grouped = keep.tile([P, QUERIES, 2, 2], BF16, name="w_grouped", align_bytes=64)
+        w_codes = keep.tile([P, QUERIES], U32, name="w_codes", align_bytes=64)
+        w_scales = keep.tile([P, QUERIES], U8, name="w_scales", align_bytes=64)
+
+        acc01 = sums.tile([P, HALVES, 2 * P], F32, name="acc01")
+        acc2 = sums.tile([P, HALVES, P], F32, name="acc2")
+        acc3 = sums.tile([P, HALVES, P], F32, name="acc3")
+        acc_of = [acc01[:, :, 0:P], acc01[:, :, P : 2 * P], acc2[:], acc3[:]]
+
+        def gather(b):
+            picked = ring.tile([P, 2, SLOTS // 2], BF16, name="picked", align_bytes=64)
+            nc.vector.tensor_copy(picked[:].rearrange("e u m -> e m u"), pools[b][:].indirect(offsets[:]))
+            turned = turn.tile([P, 2, P], F32, name="turned")
+            for u in range(2):
+                nc.tensor.transpose(turned[:, u, :], picked[:, u, :].bitcast(F32), ident[:])
+            return turned
+
+        def regroup(turned):
+            grouped = ring.tile([P, P, 2], F32, name="grouped", align_bytes=64)
+            nc.scalar.copy(grouped[:], turned[:].rearrange("p u e -> p e u"))
+            return grouped
+
+        def multiply(b, grouped):
+            codes = ring.tile([P, P], U32, name="codes", align_bytes=64)
+            scales = ring.tile([P, P], U8, name="scales", align_bytes=64)
+            nc.vector.quantize_mx(
+                out=codes[:].bitcast(FP8X4),
+                scales=scales[:],
+                in_=grouped[:].rearrange("p e u -> p (e u)").bitcast(BF16),
+            )
+            for h in range(HALVES):
+                nc.tensor.matmul_mx(
+                    out=acc_of[b][:, h, :],
+                    lhsT=w_codes[:, h * P : (h + 1) * P].bitcast(FP8X4),
+                    lhsT_scale=w_scales[:, h * P : (h + 1) * P],
+                    rhs=codes[:].bitcast(FP8X4),
+                    rhs_scale=scales[:],
+                    start=True,
+                    stop=True,
+                )
+
+        def subtract(acc, target, width, name):
+            diff = keep.tile([P, HALVES, width], F32, name=name)
+            nc.vector.tensor_tensor(diff[:], acc, target, ALU.subtract)
+            return diff
+
+        def finish(diff, first, width, name):
+            result = keep.tile([P, HALVES, width], F32, name=name)
+            nc.scalar.activation(result[:], diff[:], ACT.Square)
+            nc.sync.dma_start(out=out_rows[:, :, first : first + width], in_=result[:])
+
+        grouped0 = regroup(gather(0))
+        nc.scalar.activation(w_grouped[:], w_raw[:].rearrange("p (s u) q -> p q u s", u=2), ACT.Copy)
+        nc.vector.quantize_mx(
+            out=w_codes[:].bitcast(FP8X4),
+            scales=w_scales[:],
+            in_=w_grouped[:].rearrange("p q u s -> p (q u s)"),
+        )
+        multiply(0, grouped0)
+        for b in (1, 2):
+            multiply(b, regroup(gather(b)))
+        grouped3 = regroup(gather(3))
+        diff01 = subtract(acc01[:], tg_sb[0][:], 2 * P, "diff01")
+        finish(diff01, 0, 2 * P, "result01")
+        multiply(3, grouped3)
+        diff2 = subtract(acc2[:], tg_sb[1][:, :, 0:P], P, "diff2")
+        finish(diff2, 2 * P, P, "result2")
+        diff3 = subtract(acc3[:], tg_sb[1][:, :, P : 2 * P], P, "diff3")
+        finish(diff3, 3 * P, P, "result3")

@@ -20,98 +20,101 @@ BLOCKS = FEATURES // P
 HALVES = QUERIES // P
 
 
+WINDOW_BYTES = TOKENS * 4
+EARLY = (BLOCKS - 1) * P
+
+
 def tile_attend_wsum_dist_f_kernel(tc, vT, wT, tg, offs, out):
     nc = tc.nc
     with ExitStack() as ctx:
         keep = ctx.enter_context(tc.tile_pool(name="keep", bufs=1))
-        ring = ctx.enter_context(tc.tile_pool(name="ring", bufs=2))
+        shared = ctx.enter_context(tc.tile_pool(name="shared", bufs=1))
         turn = ctx.enter_context(tc.psum_pool(name="turn", bufs=2))
         sums = ctx.enter_context(tc.psum_pool(name="sums", bufs=1))
 
         offsets = keep.tile([P, SLOTS // 16], U16, name="offsets")
-        pools = [keep.tile([P, TOKENS], F32, name="pool%d" % b) for b in range(BLOCKS)]
+        windows = [
+            shared.tile([P, TOKENS], F32, name="window%d" % b, offset=b * WINDOW_BYTES, align_bytes=64)
+            for b in range(BLOCKS)
+        ]
         w_raw = keep.tile([P, 4, QUERIES], F32, name="w_raw")
-        tg_sb = [keep.tile([P, HALVES, 2 * P], F32, name="tg%d" % c) for c in range(2)]
-        tg_rows = tg[0].rearrange("(h p) e -> p h e", p=P)
-        out_rows = out[0].rearrange("(h p) e -> p h e", p=P)
+        targets = [keep.tile([P, FEATURES], F32, name="target%d" % h) for h in range(HALVES)]
 
-        nc.sync.dma_start(out=pools[0][:], in_=vT[0:P, :])
+        nc.sync.dma_start(out=windows[0][:], in_=vT[0:P, :])
         nc.sync.dma_start(offsets[:], offs)
         nc.sync.dma_start(out=w_raw[:], in_=wT[0].rearrange("(p j) q -> p j q", j=4))
         for b in range(1, BLOCKS):
-            nc.sync.dma_start(out=pools[b][:], in_=vT[b * P : (b + 1) * P, :])
-        for c in range(2):
-            nc.sync.dma_start(out=tg_sb[c][:], in_=tg_rows[:, :, c * 2 * P : (c + 1) * 2 * P])
+            nc.sync.dma_start(out=windows[b][:], in_=vT[b * P : (b + 1) * P, :])
+        for h in range(HALVES):
+            nc.sync.dma_start(out=targets[h][:], in_=tg[0, h * P : (h + 1) * P, :])
 
+        ident_made = keep.tile([P, P], F32, name="ident_made")
+        make_identity(nc, ident_made[:])
         ident = keep.tile([P, P], F32, name="ident")
-        make_identity(nc, ident[:])
-
-        w_grouped = keep.tile([P, QUERIES, 2, 2], BF16, name="w_grouped", align_bytes=64)
-        w_codes = keep.tile([P, QUERIES], U32, name="w_codes", align_bytes=64)
-        w_scales = keep.tile([P, QUERIES], U8, name="w_scales", align_bytes=64)
-
-        acc01 = sums.tile([P, HALVES, 2 * P], F32, name="acc01")
-        acc2 = sums.tile([P, HALVES, P], F32, name="acc2")
-        acc3 = sums.tile([P, HALVES, P], F32, name="acc3")
-        acc_of = [acc01[:, :, 0:P], acc01[:, :, P : 2 * P], acc2[:], acc3[:]]
+        nc.scalar.activation(ident[:], ident_made[:], ACT.Copy)
 
         def gather(b):
-            picked = ring.tile([P, 2, SLOTS // 2], BF16, name="picked", align_bytes=64)
-            nc.vector.tensor_copy(picked[:].rearrange("e u m -> e m u"), pools[b][:].indirect(offsets[:]))
+            picked = keep.tile([P, 2, SLOTS // 2], BF16, name="picked%d" % b, align_bytes=64)
+            nc.vector.tensor_copy(picked[:].rearrange("e u m -> e m u"), windows[b][:].indirect(offsets[:]))
             turned = turn.tile([P, 2, P], F32, name="turned")
             for u in range(2):
                 nc.tensor.transpose(turned[:, u, :], picked[:, u, :].bitcast(F32), ident[:])
-            return turned
-
-        def regroup(turned):
-            grouped = ring.tile([P, P, 2], F32, name="grouped", align_bytes=64)
+            grouped = keep.tile([P, P, 2], F32, name="grouped%d" % b, align_bytes=64)
             nc.scalar.copy(grouped[:], turned[:].rearrange("p u e -> p e u"))
-            return grouped
+            return grouped[:].rearrange("p e u -> p (e u)").bitcast(BF16)
 
-        def multiply(b, grouped):
-            codes = ring.tile([P, P], U32, name="codes", align_bytes=64)
-            scales = ring.tile([P, P], U8, name="scales", align_bytes=64)
-            nc.vector.quantize_mx(
-                out=codes[:].bitcast(FP8X4),
-                scales=scales[:],
-                in_=grouped[:].rearrange("p e u -> p (e u)").bitcast(BF16),
+        def quantize(grouped, name, offset):
+            codes = shared.tile([P, P], U32, name="codes_" + name, offset=offset, align_bytes=64)
+            scales = keep.tile([P, P], U8, name="scales_" + name, align_bytes=64)
+            nc.vector.quantize_mx(out=codes[:].bitcast(FP8X4), scales=scales[:], in_=grouped)
+            return codes, scales
+
+        def multiply(acc, w, v):
+            nc.tensor.matmul_mx(
+                out=acc,
+                lhsT=w[0][:].bitcast(FP8X4),
+                lhsT_scale=w[1][:],
+                rhs=v[0][:].bitcast(FP8X4),
+                rhs_scale=v[1][:],
+                start=True,
+                stop=True,
             )
-            for h in range(HALVES):
-                nc.tensor.matmul_mx(
-                    out=acc_of[b][:, h, :],
-                    lhsT=w_codes[:, h * P : (h + 1) * P].bitcast(FP8X4),
-                    lhsT_scale=w_scales[:, h * P : (h + 1) * P],
-                    rhs=codes[:].bitcast(FP8X4),
-                    rhs_scale=scales[:],
-                    start=True,
-                    stop=True,
-                )
 
-        def subtract(acc, target, width, name):
-            diff = keep.tile([P, HALVES, width], F32, name=name)
-            nc.vector.tensor_tensor(diff[:], acc, target, ALU.subtract)
-            return diff
-
-        def finish(diff, first, width, name):
-            result = keep.tile([P, HALVES, width], F32, name=name)
+        def finish(acc, h, first, width, offset):
+            name = "%d_%d" % (h, first)
+            diff = shared.tile([P, width], F32, name="diff" + name, offset=offset, align_bytes=64)
+            nc.vector.tensor_tensor(diff[:], acc, targets[h][:, first : first + width], ALU.subtract)
+            result = keep.tile([P, width], F32, name="result" + name)
             nc.scalar.activation(result[:], diff[:], ACT.Square)
-            nc.sync.dma_start(out=out_rows[:, :, first : first + width], in_=result[:])
+            nc.sync.dma_start(out=out[0, h * P : (h + 1) * P, first : first + width], in_=result[:])
 
-        grouped0 = regroup(gather(0))
-        nc.scalar.activation(w_grouped[:], w_raw[:].rearrange("p (s u) q -> p q u s", u=2), ACT.Copy)
-        nc.vector.quantize_mx(
-            out=w_codes[:].bitcast(FP8X4),
-            scales=w_scales[:],
-            in_=w_grouped[:].rearrange("p q u s -> p (q u s)"),
-        )
-        multiply(0, grouped0)
-        for b in (1, 2):
-            multiply(b, regroup(gather(b)))
-        grouped3 = regroup(gather(3))
-        diff01 = subtract(acc01[:], tg_sb[0][:], 2 * P, "diff01")
-        finish(diff01, 0, 2 * P, "result01")
-        multiply(3, grouped3)
-        diff2 = subtract(acc2[:], tg_sb[1][:, :, 0:P], P, "diff2")
-        finish(diff2, 2 * P, P, "result2")
-        diff3 = subtract(acc3[:], tg_sb[1][:, :, P : 2 * P], P, "diff3")
-        finish(diff3, 3 * P, P, "result3")
+        def weights(offset):
+            w_view = w_raw[:].rearrange("p (s u) q -> p q u s", u=2)
+            w_grouped = [keep.tile([P, P, 2, 2], BF16, name="w_grouped%d" % h, align_bytes=64) for h in range(HALVES)]
+            nc.vector.tensor_copy(w_grouped[0][:], w_view[:, 0:P])
+            nc.scalar.copy(w_grouped[1][:], w_view[:, P : 2 * P])
+            return [
+                quantize(w_grouped[h][:].rearrange("p q u s -> p (q u s)"), "w%d" % h, offset + 512 * h)
+                for h in range(HALVES)
+            ]
+
+        acc_early = [sums.tile([P, EARLY], F32, name="acc_early%d" % h) for h in range(HALVES)]
+        acc_last = [sums.tile([P, P], F32, name="acc_last%d" % h) for h in range(HALVES)]
+        last_window = (BLOCKS - 1) * WINDOW_BYTES
+        free = BLOCKS * WINDOW_BYTES
+
+        grouped = [gather(0)]
+        v = []
+        w = weights(free + 512)
+        for b in range(1, BLOCKS):
+            grouped.append(gather(b))
+            v.append(quantize(grouped[b - 1], "v%d" % (b - 1), b * WINDOW_BYTES))
+            for h in range(HALVES):
+                multiply(acc_early[h][:, (b - 1) * P : b * P], w[h], v[b - 1])
+        finish(acc_early[0][:], 0, 0, EARLY, last_window + 1024)
+        v.append(quantize(grouped[BLOCKS - 1], "v3", free))
+        for h in range(HALVES):
+            multiply(acc_last[h][:], w[h], v[BLOCKS - 1])
+        finish(acc_early[1][:], 1, 0, EARLY, last_window + 1024 + 2048)
+        for h in range(HALVES):
+            finish(acc_last[h][:], h, EARLY, P, free + 2048 + 512 * h)

@@ -37,14 +37,15 @@ def tile_attend_wsum_dist_f_kernel(tc, vT, wT, tg, offs, out):
             shared.tile([P, TOKENS], F32, name="window%d" % b, offset=b * WINDOW_BYTES, align_bytes=64)
             for b in range(BLOCKS)
         ]
-        w_raw = keep.tile([P, 4, QUERIES], F32, name="w_raw")
+        w_offset = BLOCKS * WINDOW_BYTES + 2048
+        w_raw = shared.tile([P, 4, QUERIES], F32, name="w_raw", offset=w_offset, align_bytes=64)
         targets = [keep.tile([P, FEATURES], F32, name="target%d" % h) for h in range(HALVES)]
 
         nc.sync.dma_start(out=windows[0][:], in_=vT[0:P, :])
         nc.sync.dma_start(offsets[:], offs)
-        nc.sync.dma_start(out=w_raw[:], in_=wT[0].rearrange("(p j) q -> p j q", j=4))
         for b in range(1, BLOCKS):
             nc.sync.dma_start(out=windows[b][:], in_=vT[b * P : (b + 1) * P, :])
+        nc.sync.dma_start(out=w_raw[:], in_=wT[0].rearrange("(p j) q -> p j q", j=4))
         for h in range(HALVES):
             nc.sync.dma_start(out=targets[h][:], in_=tg[0, h * P : (h + 1) * P, :])
 
@@ -59,7 +60,11 @@ def tile_attend_wsum_dist_f_kernel(tc, vT, wT, tg, offs, out):
             turned = turn.tile([P, 2, P], F32, name="turned")
             for u in range(2):
                 nc.tensor.transpose(turned[:, u, :], picked[:, u, :].bitcast(F32), ident[:])
-            grouped = keep.tile([P, P, 2], F32, name="grouped%d" % b, align_bytes=64)
+            return turned
+
+        def regroup(b, turned):
+            place = w_offset if b == BLOCKS - 1 else w_offset + 4096 + 1024 * b
+            grouped = shared.tile([P, P, 2], F32, name="grouped%d" % b, offset=place, align_bytes=64)
             nc.scalar.copy(grouped[:], turned[:].rearrange("p u e -> p e u"))
             return grouped[:].rearrange("p e u -> p (e u)").bitcast(BF16)
 
@@ -80,14 +85,6 @@ def tile_attend_wsum_dist_f_kernel(tc, vT, wT, tg, offs, out):
                 stop=True,
             )
 
-        def finish(acc, h, first, width, offset):
-            name = "%d_%d" % (h, first)
-            diff = shared.tile([P, width], F32, name="diff" + name, offset=offset, align_bytes=64)
-            nc.vector.tensor_tensor(diff[:], acc, targets[h][:, first : first + width], ALU.subtract)
-            result = keep.tile([P, width], F32, name="result" + name)
-            nc.scalar.activation(result[:], diff[:], ACT.Square)
-            nc.sync.dma_start(out=out[0, h * P : (h + 1) * P, first : first + width], in_=result[:])
-
         def weights(offset):
             w_view = w_raw[:].rearrange("p (s u) q -> p q u s", u=2)
             w_grouped = [keep.tile([P, P, 2, 2], BF16, name="w_grouped%d" % h, align_bytes=64) for h in range(HALVES)]
@@ -98,23 +95,36 @@ def tile_attend_wsum_dist_f_kernel(tc, vT, wT, tg, offs, out):
                 for h in range(HALVES)
             ]
 
-        acc_early = [sums.tile([P, EARLY], F32, name="acc_early%d" % h) for h in range(HALVES)]
-        acc_last = [sums.tile([P, P], F32, name="acc_last%d" % h) for h in range(HALVES)]
-        last_window = (BLOCKS - 1) * WINDOW_BYTES
         free = BLOCKS * WINDOW_BYTES
-
-        grouped = [gather(0)]
+        turned = gather(0)
         v = []
-        w = weights(free + 512)
         for b in range(1, BLOCKS):
-            grouped.append(gather(b))
-            v.append(quantize(grouped[b - 1], "v%d" % (b - 1), b * WINDOW_BYTES))
-            for h in range(HALVES):
-                multiply(acc_early[h][:, (b - 1) * P : b * P], w[h], v[b - 1])
-        finish(acc_early[0][:], 0, 0, EARLY, last_window + 1024)
-        v.append(quantize(grouped[BLOCKS - 1], "v3", free))
-        for h in range(HALVES):
-            multiply(acc_last[h][:], w[h], v[BLOCKS - 1])
-        finish(acc_early[1][:], 1, 0, EARLY, last_window + 1024 + 2048)
-        for h in range(HALVES):
-            finish(acc_last[h][:], h, EARLY, P, free + 2048 + 512 * h)
+            grouped = regroup(b - 1, turned)
+            turned = gather(b)
+            v.append(quantize(grouped, "v%d" % (b - 1), b * WINDOW_BYTES))
+        w = weights(free + 512)
+        v.append(quantize(regroup(BLOCKS - 1, turned), "v3", free))
+
+        stores = [
+            (0, [[0], [1, 2]]),
+            (1, [[0, 1], [2]]),
+            (0, [[3]]),
+            (1, [[3]]),
+        ]
+        banks = {}
+        for h, pieces in stores:
+            for piece in pieces:
+                acc = sums.tile([P, len(piece) * P], F32, name="acc%d_%d" % (h, piece[0]))
+                banks[h, piece[0]] = acc
+                for i, b in enumerate(piece):
+                    multiply(acc[:, i * P : (i + 1) * P], w[h], v[b])
+        for h, pieces in stores:
+            first = pieces[0][0] * P
+            width = sum(len(piece) for piece in pieces) * P
+            result = keep.tile([P, width], F32, name="result%d_%d" % (h, first))
+            for piece in pieces:
+                lo, hi = piece[0] * P, (piece[-1] + 1) * P
+                diff = keep.tile([P, hi - lo], F32, name="diff%d_%d" % (h, lo))
+                nc.vector.tensor_tensor(diff[:], banks[h, piece[0]][:], targets[h][:, lo:hi], ALU.subtract)
+                nc.scalar.activation(result[:, lo - first : hi - first], diff[:], ACT.Square)
+            nc.sync.dma_start(out=out[0, h * P : (h + 1) * P, first : first + width], in_=result[:])

@@ -86,10 +86,11 @@ def tile_attend_wsum_dist_f_kernel(tc, vT, wT, tg, offs, out):
             )
 
         def weights(offset):
-            w_view = w_raw[:].rearrange("p (s u) q -> p q u s", u=2)
+            w_view = w_raw[:].rearrange("p (s u) (c i) -> p c u s i", u=2, i=4)
             w_grouped = [keep.tile([P, P, 2, 2], BF16, name="w_grouped%d" % h, align_bytes=64) for h in range(HALVES)]
-            nc.vector.tensor_copy(w_grouped[0][:], w_view[:, 0:P])
-            nc.scalar.copy(w_grouped[1][:], w_view[:, P : 2 * P])
+            order = "p (c i) u s -> p c u s i"
+            nc.vector.tensor_copy(w_grouped[0][:].rearrange(order, i=4), w_view[:, 0 : P // 4])
+            nc.scalar.copy(w_grouped[1][:].rearrange(order, i=4), w_view[:, P // 4 : P // 2])
             return [
                 quantize(w_grouped[h][:].rearrange("p q u s -> p (q u s)"), "w%d" % h, offset + 512 * h)
                 for h in range(HALVES)
@@ -106,8 +107,10 @@ def tile_attend_wsum_dist_f_kernel(tc, vT, wT, tg, offs, out):
         v.append(quantize(regroup(BLOCKS - 1, turned), "v3", free))
 
         stores = [
-            (0, [[0], [1, 2]]),
-            (1, [[0, 1], [2]]),
+            (0, [[0]]),
+            (0, [[1, 2]]),
+            (1, [[0, 1]]),
+            (1, [[2]]),
             (0, [[3]]),
             (1, [[3]]),
         ]

from contextlib import ExitStack

import concourse.mybir as mybir
from concourse.masks import make_identity

SLOTS, TOKENS, QUERIES, FEATURES = 512, 2048, 256, 512
FLOPS = 2 * QUERIES * SLOTS * FEATURES

F32 = mybir.dt.float32
BF16 = mybir.dt.bfloat16
U32 = mybir.dt.uint32
U16 = mybir.dt.uint16
U8 = mybir.dt.uint8
FP8X4 = mybir.dt.float8_e4m3fn_x4
ACT = mybir.ActivationFunctionType
ALU = mybir.AluOpType

P = 128
BLOCKS = FEATURES // P
HALVES = QUERIES // P


WINDOW_BYTES = TOKENS * 4
EARLY = (BLOCKS - 1) * P


def tile_attend_wsum_dist_f_kernel(tc, vT, wT, tg, offs, out):
    nc = tc.nc
    with ExitStack() as ctx:
        keep = ctx.enter_context(tc.tile_pool(name="keep", bufs=1))
        shared = ctx.enter_context(tc.tile_pool(name="shared", bufs=1))
        turn = ctx.enter_context(tc.psum_pool(name="turn", bufs=2))
        sums = ctx.enter_context(tc.psum_pool(name="sums", bufs=1))

        offsets = keep.tile([P, SLOTS // 16], U16, name="offsets")
        windows = [
            shared.tile([P, TOKENS], F32, name="window%d" % b, offset=b * WINDOW_BYTES, align_bytes=64)
            for b in range(BLOCKS)
        ]
        w_offset = BLOCKS * WINDOW_BYTES + 2048
        w_raw = shared.tile([P, 4, QUERIES], F32, name="w_raw", offset=w_offset, align_bytes=64)
        targets = [keep.tile([P, FEATURES], F32, name="target%d" % h) for h in range(HALVES)]

        nc.sync.dma_start(out=windows[0][:], in_=vT[0:P, :])
        nc.sync.dma_start(offsets[:], offs)
        for b in range(1, BLOCKS):
            nc.sync.dma_start(out=windows[b][:], in_=vT[b * P : (b + 1) * P, :])
        nc.sync.dma_start(out=w_raw[:], in_=wT[0].rearrange("(p j) q -> p j q", j=4))
        for h in range(HALVES):
            nc.sync.dma_start(out=targets[h][:], in_=tg[0, h * P : (h + 1) * P, :])

        ident_made = keep.tile([P, P], F32, name="ident_made")
        make_identity(nc, ident_made[:])
        ident = keep.tile([P, P], F32, name="ident")
        nc.scalar.activation(ident[:], ident_made[:], ACT.Copy)

        def gather(b):
            picked = keep.tile([P, 2, SLOTS // 2], BF16, name="picked%d" % b, align_bytes=64)
            nc.vector.tensor_copy(picked[:].rearrange("e u m -> e m u"), windows[b][:].indirect(offsets[:]))
            turned = turn.tile([P, 2, P], F32, name="turned")
            for u in range(2):
                nc.tensor.transpose(turned[:, u, :], picked[:, u, :].bitcast(F32), ident[:])
            return turned

        def regroup(b, turned):
            place = w_offset if b == BLOCKS - 1 else w_offset + 4096 + 1024 * b
            grouped = shared.tile([P, P, 2], F32, name="grouped%d" % b, offset=place, align_bytes=64)
            nc.scalar.copy(grouped[:], turned[:].rearrange("p u e -> p e u"))
            return grouped[:].rearrange("p e u -> p (e u)").bitcast(BF16)

        def quantize(grouped, name, offset):
            codes = shared.tile([P, P], U32, name="codes_" + name, offset=offset, align_bytes=64)
            scales = keep.tile([P, P], U8, name="scales_" + name, align_bytes=64)
            nc.vector.quantize_mx(out=codes[:].bitcast(FP8X4), scales=scales[:], in_=grouped)
            return codes, scales

        def multiply(acc, w, v):
            nc.tensor.matmul_mx(
                out=acc,
                lhsT=w[0][:].bitcast(FP8X4),
                lhsT_scale=w[1][:],
                rhs=v[0][:].bitcast(FP8X4),
                rhs_scale=v[1][:],
                start=True,
                stop=True,
            )

        def weights(offset):
            w_view = w_raw[:].rearrange("p (s u) (c i) -> p c u s i", u=2, i=4)
            w_grouped = [keep.tile([P, P, 2, 2], BF16, name="w_grouped%d" % h, align_bytes=64) for h in range(HALVES)]
            order = "p (c i) u s -> p c u s i"
            nc.vector.tensor_copy(w_grouped[0][:].rearrange(order, i=4), w_view[:, 0 : P // 4])
            nc.scalar.copy(w_grouped[1][:].rearrange(order, i=4), w_view[:, P // 4 : P // 2])
            return [
                quantize(w_grouped[h][:].rearrange("p q u s -> p (q u s)"), "w%d" % h, offset + 512 * h)
                for h in range(HALVES)
            ]

        free = BLOCKS * WINDOW_BYTES
        turned = gather(0)
        v = []
        for b in range(1, BLOCKS):
            grouped = regroup(b - 1, turned)
            turned = gather(b)
            v.append(quantize(grouped, "v%d" % (b - 1), b * WINDOW_BYTES))
        w = weights(free + 512)
        v.append(quantize(regroup(BLOCKS - 1, turned), "v3", free))

        stores = [
            (0, [[0]]),
            (0, [[1, 2]]),
            (1, [[0, 1]]),
            (1, [[2]]),
            (0, [[3]]),
            (1, [[3]]),
        ]
        banks = {}
        for h, pieces in stores:
            for piece in pieces:
                acc = sums.tile([P, len(piece) * P], F32, name="acc%d_%d" % (h, piece[0]))
                banks[h, piece[0]] = acc
                for i, b in enumerate(piece):
                    multiply(acc[:, i * P : (i + 1) * P], w[h], v[b])
        for h, pieces in stores:
            first = pieces[0][0] * P
            width = sum(len(piece) for piece in pieces) * P
            result = keep.tile([P, width], F32, name="result%d_%d" % (h, first))
            for piece in pieces:
                lo, hi = piece[0] * P, (piece[-1] + 1) * P
                diff = keep.tile([P, hi - lo], F32, name="diff%d_%d" % (h, lo))
                nc.vector.tensor_tensor(diff[:], banks[h, piece[0]][:], targets[h][:, lo:hi], ALU.subtract)
                nc.scalar.activation(result[:, lo - first : hi - first], diff[:], ACT.Square)
            nc.sync.dma_start(out=out[0, h * P : (h + 1) * P, first : first + width], in_=result[:])
